import numpy as np, ml_dtypes
CORES = [8,80,112,136,208,240,264,336,368,392,464,496]
N = 12
TK = 64
def gelu(z): return 0.5 * z * (1.0 + np.tanh(0.7978845608028654 * (z + 0.044715 * z ** 3)))
def setup_inputs(rng):
    return {"x": rng.standard_normal((N, 128, TK), dtype=np.float32).astype(ml_dtypes.bfloat16), "w1": (rng.standard_normal((N, 128, 128), dtype=np.float32) / 8).astype(ml_dtypes.bfloat16), "w2": (rng.standard_normal((N, 128, 128), dtype=np.float32) / 8).astype(ml_dtypes.bfloat16)}
def setup_inputs_big(rng):
    d = setup_inputs(rng)
    for k in ("x",): d[k] = (d[k].astype(np.float32) * 1024.0).astype(d[k].dtype)
    return d
def setup_inputs_small(rng):
    d = setup_inputs(rng)
    for k in ("x",): d[k] = (d[k].astype(np.float32) * (1 / 1024.0)).astype(d[k].dtype)
    return d
def setup_inputs_apart(rng):
    d = setup_inputs(rng)
    f = (10.0 ** rng.permutation(np.linspace(-1.5, 1.5, N))).astype(np.float32).reshape(N, 1, 1)
    for k in ("x",): d[k] = (d[k].astype(np.float32) * f).astype(d[k].dtype)
    return d
def reference(x, w1, w2):
    X, W1, W2 = x.astype(np.float64), w1.astype(np.float64), w2.astype(np.float64)
    y = np.zeros((N, 128, TK))
    for r in range(N):
        for j in range(N):
            y[r] += W2[j].T @ (gelu(W1[j].T @ X[r]))
    return {"y": y.astype(ml_dtypes.bfloat16)}

@@ -1,0 +1,197 @@
+from concourse.bass import DstId, RemoteDMATransfer
+from concourse.mybir import ActivationFunctionType
+
+N, TK, D = 12, 64, 128
+NSIM = 512
+W = 2 * D
+NB = 4
+KEEP = 5
+SAME, CROSS, FAR = 3, 2, 3
+NE_HOP1, NE_KEEP, NE_LAST = 8, 8, 8
+
+SCRATCH = {
+    "wd": ("dram", [D, W], "bfloat16"),
+    "wall": ("sbuf", [D, N * W], "bfloat16"),
+    "xs": ("sbuf", [D, TK], "bfloat16"),
+    "hs": ("sbuf", [D, N * TK], "bfloat16"),
+    "ys": ("sbuf", [D, TK], "bfloat16"),
+    "yp": ("psum", [D, 512], "float32"),
+}
+for _b in range(NB):
+    SCRATCH["hp%d" % _b] = ("psum", [D, 512], "float32")
+
+SEMAPHORES = (["ldw", "ldo", "snt", "acc", "cp", "st"] + ["a%d" % j for j in range(N)]
+              + ["p%d" % k for k in range(N)] + ["c%d" % k for k in range(N)])
+
+_CACHE = {}
+
+
+def _perms(a):
+    if len(a) <= 1:
+        return [list(a)]
+    return [[a[i]] + p for i in range(len(a)) for p in _perms(a[:i] + a[i + 1:])]
+
+
+def _stagger(ds, seen, tag):
+    best = min(_perms(ds), key=lambda p: sum(seen.get((d, tag, i), 0) for i, d in enumerate(p)))
+    for i, d in enumerate(best):
+        seen[(d, tag, i)] = seen.get((d, tag, i), 0) + 1
+    return best
+
+
+def _plan(cores, topo):
+    ranks = list(cores)
+    taken = set(ranks)
+    seen = {}
+
+    def place(c):
+        return (topo.host(c), topo.chip(c))
+
+    def rk(c):
+        return topo.rack(topo.host(c))
+
+    groups = []
+    for j, s in enumerate(ranks):
+        rot = ranks[j + 1:] + ranks[:j]
+        can = sorted([d for d in rot if topo.may_write(s, d)], key=lambda d: rk(d) == rk(s))
+        keep = _stagger(can[:KEEP], seen, "rank")
+        rest = [d for d in rot if d not in keep]
+        sites = {}
+        for c in range(NSIM):
+            if c not in taken and topo.chip(c) == topo.chip(s) and topo.may_write(s, c):
+                sites.setdefault(topo.host(c), []).append(c)
+        home = topo.host(s)
+        opts = {}
+        for d in rest:
+            if rk(d) == rk(s):
+                opts[d] = [home]
+            else:
+                opts[d] = [h for h in sites if h != home and any(topo.may_write(c, d) for c in sites[h])]
+        load = {h: [] for h in sites}
+        for d in sorted(rest, key=lambda d: len(opts[d])):
+            h = min(opts[d], key=lambda h: (len(load[h]), topo.rack(h) != rk(d)))
+            load[h].append(d)
+        chunks = []
+        for h, ds in load.items():
+            if h == home:
+                a = [d for d in ds if d in can]
+                b = [d for d in ds if d not in can]
+                chunks += [(h, a[k:k + SAME]) for k in range(0, len(a), SAME)]
+                chunks += [(h, b[k:k + CROSS]) for k in range(0, len(b), CROSS)]
+            else:
+                chunks += [(h, ds[k:k + FAR]) for k in range(0, len(ds), FAR)]
+        groups.append((keep, chunks))
+
+    arrive = {}
+    routes = []
+    for j, s in enumerate(ranks):
+        keep, chunks = groups[j]
+        helpers = []
+        for h, ch in chunks:
+            cand = [c for c in range(NSIM) if c not in taken and topo.host(c) == h and topo.chip(c) == topo.chip(s)
+                    and topo.may_write(s, c) and all(topo.may_write(c, d) for d in ch)]
+            m = min(cand, key=lambda c: (sum(arrive.get(place(d) + (topo.die(c),), 0) for d in ch),
+                                         sum(topo.may_write(c, d) for d in ranks), c))
+            taken.add(m)
+            for d in ch:
+                key = place(d) + (topo.die(m),)
+                arrive[key] = arrive.get(key, 0) + 1
+            helpers.append((m, _stagger(ch, seen, topo.die(m))))
+        helpers.sort(key=lambda t: (-len(t[1]), place(t[0]) == place(s)))
+        routes.append((keep, helpers))
+    return routes
+
+
+def _engines(topo, src, dsts, n):
+    allowed = topo.mask(src, dsts[0])
+    for d in dsts[1:]:
+        allowed &= topo.mask(src, d)
+    out, b, k = 0, 0, 0
+    while k < n:
+        if (allowed >> b) & 1:
+            out |= 1 << b
+            k += 1
+        b += 1
+    return out
+
+
+def _send(g, T, topo, core, dsts, out_ap, sem, n):
+    ids = []
+    for d in dsts:
+        rid, pid = topo.addr(d, core)
+        ids.append(DstId(rid=rid, pnc=pid))
+    g.remote_dma_fused([RemoteDMATransfer(dst_ids=ids, dma_engine_mask=_engines(topo, core, dsts, n), remote_sem=sem,
+                                          srcs=[T.wd[:]], dsts=[out_ap for _ in dsts], alu_op=0)],
+                       local_sem=T.sem.snt)
+    return n
+
+
+def rank_program(g, core, T, topo):
+    if "routes" not in _CACHE:
+        _CACHE["routes"] = _plan(T.cores, topo)
+    routes = _CACHE["routes"]
+    rank = T.rank_of(core)
+
+    if rank is None:
+        for j, (keep, helpers) in enumerate(routes):
+            for m, ch in helpers:
+                if m == core:
+                    sem = T.sem["a%d" % j]
+                    g.wait_ge(sem, NE_HOP1)
+                    n = _send(g, T, topo, core, ch, T.wall[:, j * W:(j + 1) * W], sem, NE_LAST)
+                    g.wait_ge(T.sem.snt, n)
+        return
+
+    me = rank
+    keep, helpers = routes[me]
+    own = T.wall[:, me * W:(me + 1) * W]
+
+    g.sync.dma_start(T.wd[:, 0:D], T.w1[:]).then_inc(T.sem.ldw, 16)
+    g.scalar.dma_start(T.wd[:, D:W], T.w2[:]).then_inc(T.sem.ldw, 16)
+    g.sync.dma_start(T.xs[:], T.x[:]).then_inc(T.sem.ldo, 16)
+    g.scalar.dma_start(T.wall[:, me * W + D:(me + 1) * W], T.w2[:]).then_inc(T.sem.ldo, 16)
+    g.sync.dma_start(T.wall[:, me * W:me * W + D], T.w1[:]).then_inc(T.sem.ldo, 16)
+
+    g.wait_ge(T.sem.ldw, 32)
+    sem = T.sem["a%d" % me]
+    sent = _send(g, T, topo, core, [m for m, _ in helpers], T.wd[:], sem, NE_HOP1)
+    if keep:
+        sent += _send(g, T, topo, core, keep, own, sem, NE_KEEP)
+
+    when, count = {}, {}
+    for j, (kp, hl) in enumerate(routes):
+        if core in kp:
+            when[j], count[j] = (1, kp.index(core), 0), NE_KEEP
+        for i, (m, ch) in enumerate(hl):
+            if core in ch:
+                when[j], count[j] = (2, ch.index(core), i), NE_LAST
+    order = [me] + sorted(when, key=lambda j: when[j])
+
+    pe, act, vec = g.tensor, g.scalar, g.vector
+
+    def second(k):
+        j = order[k]
+        pe.wait_ge(T.sem["c%d" % k], 1)
+        pe.matmul(T.yp[:, 0:TK], T.wall[:, j * W + D:(j + 1) * W], T.hs[:, k * TK:(k + 1) * TK],
+                  k == 0, k == N - 1).then_inc(T.sem.acc, 1)
+
+    for k, j in enumerate(order):
+        if k == 0:
+            pe.wait_ge(T.sem.ldo, 48)
+        else:
+            pe.wait_ge(T.sem["a%d" % j], count[j])
+        hp = T["hp%d" % (k % NB)]
+        pe.matmul(hp[:, 0:TK], T.wall[:, j * W:j * W + D], T.xs[:], True, True).then_inc(T.sem["p%d" % k], 1)
+        act.wait_ge(T.sem["p%d" % k], 1)
+        act.activation(T.hs[:, k * TK:(k + 1) * TK], hp[:, 0:TK],
+                       ActivationFunctionType.Gelu_apprx_tanh).then_inc(T.sem["c%d" % k], 1)
+        if k >= 1:
+            second(k - 1)
+    second(N - 1)
+
+    vec.wait_ge(T.sem.acc, N)
+    vec.tensor_copy(T.ys[:], T.yp[:, 0:TK]).then_inc(T.sem.cp, 1)
+    g.sync.wait_ge(T.sem.cp, 1)
+    g.sync.dma_start(T.y[:], T.ys[:]).then_inc(T.sem.st, 16)
+    g.sync.wait_ge(T.sem.st, 16)
+    g.wait_ge(T.sem.snt, sent)

@@ -1,105 +1,82 @@
 from concourse.bass import DstId, RemoteDMATransfer
-from concourse.mybir import ActivationFunctionType
+from concourse.mybir import ActivationFunctionType, AluOpType
 
 N, TK, D = 12, 64, 128
 NSIM = 512
 W = 2 * D
-NB = 4
-KEEP = 5
-SAME, CROSS, FAR = 3, 2, 3
-NE_HOP1, NE_KEEP, NE_LAST = 8, 8, 8
+G = 6
+NBH, NBY = 5, 3
+NE = 8
 
 SCRATCH = {
-    "wd": ("dram", [D, W], "bfloat16"),
-    "wall": ("sbuf", [D, N * W], "bfloat16"),
     "xs": ("sbuf", [D, TK], "bfloat16"),
-    "hs": ("sbuf", [D, N * TK], "bfloat16"),
+    "ws": ("sbuf", [D, W], "bfloat16"),
+    "yin": ("sbuf", [D, G * TK], "bfloat16"),
+    "acc": ("sbuf", [D, (G - 2) * TK], "float32"),
     "ys": ("sbuf", [D, TK], "bfloat16"),
-    "yp": ("psum", [D, 512], "float32"),
+    "xall": ("sbuf", [D, G * TK], "bfloat16"),
+    "wts": ("sbuf", [D, 2 * W], "bfloat16"),
+    "hs": ("sbuf", [D, G * 2 * TK], "bfloat16"),
+    "yo": ("sbuf", [D, G * TK], "bfloat16"),
 }
-for _b in range(NB):
+for _b in range(NBH):
     SCRATCH["hp%d" % _b] = ("psum", [D, 512], "float32")
+for _b in range(NBY):
+    SCRATCH["yp%d" % _b] = ("psum", [D, 512], "float32")
 
-SEMAPHORES = (["ldw", "ldo", "snt", "acc", "cp", "st"] + ["a%d" % j for j in range(N)]
-              + ["p%d" % k for k in range(N)] + ["c%d" % k for k in range(N)])
+SEMAPHORES = (["ldx", "ldw", "snt", "st", "w0", "w1"] + ["xa%d" % a for a in range(G)] + ["ya%d" % a for a in range(G)]
+              + ["p%d" % u for u in range(G + 1)] + ["c%d" % k for k in range(G)] + ["q%d" % k for k in range(G)]
+              + ["v%d" % k for k in range(G)] + ["s%d" % k for k in range(G)])
 
 _CACHE = {}
 
 
-def _perms(a):
-    if len(a) <= 1:
-        return [list(a)]
-    return [[a[i]] + p for i in range(len(a)) for p in _perms(a[:i] + a[i + 1:])]
-
-
-def _stagger(ds, seen, tag):
-    best = min(_perms(ds), key=lambda p: sum(seen.get((d, tag, i), 0) for i, d in enumerate(p)))
-    for i, d in enumerate(best):
-        seen[(d, tag, i)] = seen.get((d, tag, i), 0) + 1
-    return best
-
-
 def _plan(cores, topo):
     ranks = list(cores)
-    taken = set(ranks)
-    seen = {}
-
-    def place(c):
-        return (topo.host(c), topo.chip(c))
 
     def rk(c):
         return topo.rack(topo.host(c))
 
-    groups = []
-    for j, s in enumerate(ranks):
-        rot = ranks[j + 1:] + ranks[:j]
-        can = sorted([d for d in rot if topo.may_write(s, d)], key=lambda d: rk(d) == rk(s))
-        keep = _stagger(can[:KEEP], seen, "rank")
-        rest = [d for d in rot if d not in keep]
-        sites = {}
-        for c in range(NSIM):
-            if c not in taken and topo.chip(c) == topo.chip(s) and topo.may_write(s, c):
-                sites.setdefault(topo.host(c), []).append(c)
-        home = topo.host(s)
-        opts = {}
-        for d in rest:
-            if rk(d) == rk(s):
-                opts[d] = [home]
-            else:
-                opts[d] = [h for h in sites if h != home and any(topo.may_write(c, d) for c in sites[h])]
-        load = {h: [] for h in sites}
-        for d in sorted(rest, key=lambda d: len(opts[d])):
-            h = min(opts[d], key=lambda h: (len(load[h]), topo.rack(h) != rk(d)))
-            load[h].append(d)
-        chunks = []
-        for h, ds in load.items():
-            if h == home:
-                a = [d for d in ds if d in can]
-                b = [d for d in ds if d not in can]
-                chunks += [(h, a[k:k + SAME]) for k in range(0, len(a), SAME)]
-                chunks += [(h, b[k:k + CROSS]) for k in range(0, len(b), CROSS)]
-            else:
-                chunks += [(h, ds[k:k + FAR]) for k in range(0, len(ds), FAR)]
-        groups.append((keep, chunks))
+    def place(c):
+        return (topo.host(c), topo.chip(c))
 
-    arrive = {}
-    routes = []
-    for j, s in enumerate(ranks):
-        keep, chunks = groups[j]
-        helpers = []
-        for h, ch in chunks:
-            cand = [c for c in range(NSIM) if c not in taken and topo.host(c) == h and topo.chip(c) == topo.chip(s)
-                    and topo.may_write(s, c) and all(topo.may_write(c, d) for d in ch)]
-            m = min(cand, key=lambda c: (sum(arrive.get(place(d) + (topo.die(c),), 0) for d in ch),
-                                         sum(topo.may_write(c, d) for d in ranks), c))
-            taken.add(m)
-            for d in ch:
-                key = place(d) + (topo.die(m),)
-                arrive[key] = arrive.get(key, 0) + 1
-            helpers.append((m, _stagger(ch, seen, topo.die(m))))
-        helpers.sort(key=lambda t: (-len(t[1]), place(t[0]) == place(s)))
-        routes.append((keep, helpers))
-    return routes
+    peers = [[k for k in range(N) if rk(ranks[k]) == rk(ranks[i])] for i in range(N)]
+    site = []
+    for i, s in enumerate(ranks):
+        cand = [c for c in range(NSIM) if place(c) == place(s) and c not in ranks
+                and all(topo.may_write(c, ranks[k]) for k in peers[i])]
+        site.append(min(cand, key=lambda c: (topo.die(c) != topo.die(s), c)))
+    partner, direct, fwd = [], [], []
+    for i, s in enumerate(ranks):
+        partner.append([k for k in range(N) if rk(ranks[k]) != rk(s) and topo.chip(ranks[k]) == topo.chip(s)
+                        and topo.may_write(s, site[k])][0])
+        a = peers[i].index(i)
+        rot = peers[i][a + 1:] + peers[i][:a]
+        direct.append([k for k in rot if topo.may_write(s, site[k])])
+        fwd.append([k for k in rot if not topo.may_write(s, site[k])])
+
+    def when(k, i):
+        if k == i:
+            return (1, 0)
+        if i in direct[k]:
+            return (1, 1 + direct[k].index(i))
+        return (2, fwd[k].index(i))
+
+    order, waves = [], []
+    for i in range(N):
+        o = sorted(peers[i], key=lambda k: when(k, i))
+        order.append(o)
+        wv = [[n for n, k in enumerate(o) if when(k, i)[0] == 1]]
+        for n, k in enumerate(o):
+            if when(k, i)[0] == 2:
+                if len(wv[-1]) and when(o[wv[-1][-1]], i) == when(k, i):
+                    wv[-1].append(n)
+                else:
+                    wv.append([n])
+        waves.append(wv)
+    sums = [sorted(peers[r], key=lambda i: (when(r, i)[0], order[i].index(r), when(r, i)[1])) for r in range(N)]
+    return {"peers": peers, "site": site, "partner": partner, "direct": direct, "fwd": fwd, "order": order,
+            "waves": waves, "sums": sums, "rack": [rk(c) for c in ranks]}
 
 
 def _engines(topo, src, dsts, n):
@@ -115,83 +92,130 @@ def _engines(topo, src, dsts, n):
     return out
 
 
-def _send(g, T, topo, core, dsts, out_ap, sem, n):
+def _send(g, T, topo, core, dsts, out_ap, in_ap, sem):
     ids = []
     for d in dsts:
         rid, pid = topo.addr(d, core)
         ids.append(DstId(rid=rid, pnc=pid))
-    g.remote_dma_fused([RemoteDMATransfer(dst_ids=ids, dma_engine_mask=_engines(topo, core, dsts, n), remote_sem=sem,
-                                          srcs=[T.wd[:]], dsts=[out_ap for _ in dsts], alu_op=0)],
+    g.remote_dma_fused([RemoteDMATransfer(dst_ids=ids, dma_engine_mask=_engines(topo, core, dsts, NE), remote_sem=sem,
+                                          srcs=[in_ap], dsts=[out_ap for _ in dsts], alu_op=0)],
                        local_sem=T.sem.snt)
-    return n
+    return NE
 
 
-def rank_program(g, core, T, topo):
-    if "routes" not in _CACHE:
-        _CACHE["routes"] = _plan(T.cores, topo)
-    routes = _CACHE["routes"]
-    rank = T.rank_of(core)
+def _rank(g, core, T, topo, P, me):
+    ranks = list(T.cores)
+    peers, site = P["peers"][me], P["site"]
+    a = peers.index(me)
 
-    if rank is None:
-        for j, (keep, helpers) in enumerate(routes):
-            for m, ch in helpers:
-                if m == core:
-                    sem = T.sem["a%d" % j]
-                    g.wait_ge(sem, NE_HOP1)
-                    n = _send(g, T, topo, core, ch, T.wall[:, j * W:(j + 1) * W], sem, NE_LAST)
-                    g.wait_ge(T.sem.snt, n)
-        return
+    g.sync.dma_start(T.xs[:], T.x[:]).then_inc(T.sem.ldx, 16)
+    g.scalar.dma_start(T.ws[:, 0:D], T.w1[:]).then_inc(T.sem.ldw, 16)
+    g.sync.dma_start(T.ws[:, D:W], T.w2[:]).then_inc(T.sem.ldw, 16)
 
-    me = rank
-    keep, helpers = routes[me]
-    own = T.wall[:, me * W:(me + 1) * W]
-
-    g.sync.dma_start(T.wd[:, 0:D], T.w1[:]).then_inc(T.sem.ldw, 16)
-    g.scalar.dma_start(T.wd[:, D:W], T.w2[:]).then_inc(T.sem.ldw, 16)
-    g.sync.dma_start(T.xs[:], T.x[:]).then_inc(T.sem.ldo, 16)
-    g.scalar.dma_start(T.wall[:, me * W + D:(me + 1) * W], T.w2[:]).then_inc(T.sem.ldo, 16)
-    g.sync.dma_start(T.wall[:, me * W:me * W + D], T.w1[:]).then_inc(T.sem.ldo, 16)
-
+    g.wait_ge(T.sem.ldx, 16)
+    sent = _send(g, T, topo, core, [site[me]] + [site[k] for k in P["direct"][me]],
+                 T.xall[:, a * TK:(a + 1) * TK], T.xs[:], T.sem["xa%d" % a])
     g.wait_ge(T.sem.ldw, 32)
-    sem = T.sem["a%d" % me]
-    sent = _send(g, T, topo, core, [m for m, _ in helpers], T.wd[:], sem, NE_HOP1)
-    if keep:
-        sent += _send(g, T, topo, core, keep, own, sem, NE_KEEP)
+    r = P["rack"][me]
+    sent += _send(g, T, topo, core, [site[me], site[P["partner"][me]]],
+                  T.wts[:, r * W:(r + 1) * W], T.ws[:], T.sem["w%d" % r])
 
-    when, count = {}, {}
-    for j, (kp, hl) in enumerate(routes):
-        if core in kp:
-            when[j], count[j] = (1, kp.index(core), 0), NE_KEEP
-        for i, (m, ch) in enumerate(hl):
-            if core in ch:
-                when[j], count[j] = (2, ch.index(core), i), NE_LAST
-    order = [me] + sorted(when, key=lambda j: when[j])
-
-    pe, act, vec = g.tensor, g.scalar, g.vector
-
-    def second(k):
-        j = order[k]
-        pe.wait_ge(T.sem["c%d" % k], 1)
-        pe.matmul(T.yp[:, 0:TK], T.wall[:, j * W + D:(j + 1) * W], T.hs[:, k * TK:(k + 1) * TK],
-                  k == 0, k == N - 1).then_inc(T.sem.acc, 1)
-
-    for k, j in enumerate(order):
-        if k == 0:
-            pe.wait_ge(T.sem.ldo, 48)
-        else:
-            pe.wait_ge(T.sem["a%d" % j], count[j])
-        hp = T["hp%d" % (k % NB)]
-        pe.matmul(hp[:, 0:TK], T.wall[:, j * W:j * W + D], T.xs[:], True, True).then_inc(T.sem["p%d" % k], 1)
-        act.wait_ge(T.sem["p%d" % k], 1)
-        act.activation(T.hs[:, k * TK:(k + 1) * TK], hp[:, 0:TK],
-                       ActivationFunctionType.Gelu_apprx_tanh).then_inc(T.sem["c%d" % k], 1)
-        if k >= 1:
-            second(k - 1)
-    second(N - 1)
-
-    vec.wait_ge(T.sem.acc, N)
-    vec.tensor_copy(T.ys[:], T.yp[:, 0:TK]).then_inc(T.sem.cp, 1)
-    g.sync.wait_ge(T.sem.cp, 1)
+    vec = g.vector
+    prev = None
+    for n, i in enumerate(P["sums"][me]):
+        b = peers.index(i)
+        part = T.yin[:, b * TK:(b + 1) * TK]
+        vec.wait_ge(T.sem["ya%d" % b], NE)
+        if n == 0:
+            prev = part
+            continue
+        if n >= 2:
+            vec.wait_ge(T.sem["s%d" % (n - 1)], 1)
+        out = T.ys[:] if n == G - 1 else T.acc[:, (n - 1) * TK:n * TK]
+        vec.tensor_tensor(out, prev, part, AluOpType.add).then_inc(T.sem["s%d" % n], 1)
+        prev = out
+    g.sync.wait_ge(T.sem["s%d" % (G - 1)], 1)
     g.sync.dma_start(T.y[:], T.ys[:]).then_inc(T.sem.st, 16)
     g.sync.wait_ge(T.sem.st, 16)
     g.wait_ge(T.sem.snt, sent)
+
+
+def _site(g, core, T, topo, P, me):
+    ranks = list(T.cores)
+    peers, site, order = P["peers"][me], P["site"], P["order"][me]
+    a = peers.index(me)
+    pe, act, vec = g.tensor, g.scalar, g.vector
+    gelu = ActivationFunctionType.Gelu_apprx_tanh
+    home = P["rack"][me]
+    slots = [home, 1 - home]
+    w1 = [T.wts[:, s * W:s * W + D] for s in slots]
+    w2 = [T.wts[:, s * W + D:(s + 1) * W] for s in slots]
+
+    g.wait_ge(T.sem["xa%d" % a], NE)
+    sent = _send(g, T, topo, core, [site[k] for k in P["fwd"][me]],
+                 T.xall[:, a * TK:(a + 1) * TK], T.xall[:, a * TK:(a + 1) * TK], T.sem["xa%d" % a])
+
+    unit = [0]
+    reader = []
+
+    def bank():
+        u = unit[0]
+        unit[0] += 1
+        if u >= NBH:
+            pe.wait_ge(*reader[u - NBH])
+        return u, T["hp%d" % (u % NBH)]
+
+    def first(k):
+        b = peers.index(order[k])
+        x = T.xall[:, b * TK:(b + 1) * TK]
+        pe.wait_ge(T.sem["xa%d" % b], NE)
+        ck = T.sem["c%d" % k]
+        if k == 0:
+            for e in range(2):
+                pe.wait_ge(T.sem["w%d" % slots[e]], NE)
+                u, hp = bank()
+                reader.append((ck, 2))
+                pe.matmul(hp[:, 0:TK], w1[e], x, True, True).then_inc(T.sem["p%d" % u], 1)
+                act.wait_ge(T.sem["p%d" % u], 1)
+                act.activation(T.hs[:, e * TK:(e + 1) * TK], hp[:, 0:TK], gelu).then_inc(ck, 1)
+        else:
+            u, hp = bank()
+            reader.append((ck, 1))
+            for e in range(2):
+                pe.matmul(hp[:, e * TK:(e + 1) * TK], w1[e], x, True, True).then_inc(T.sem["p%d" % u], 1)
+            act.wait_ge(T.sem["p%d" % u], 2)
+            act.activation(T.hs[:, 2 * k * TK:(2 * k + 2) * TK], hp[:, 0:2 * TK], gelu).then_inc(ck, 1)
+
+    def second(k):
+        pe.wait_ge(T.sem["c%d" % k], 2 if k == 0 else 1)
+        if k >= NBY:
+            pe.wait_ge(T.sem["v%d" % (k - NBY)], 1)
+        yp = T["yp%d" % (k % NBY)]
+        for e in range(2):
+            pe.matmul(yp[:, 0:TK], w2[e], T.hs[:, (2 * k + e) * TK:(2 * k + e + 1) * TK],
+                      e == 0, e == 1).then_inc(T.sem["q%d" % k], 1)
+        vec.wait_ge(T.sem["q%d" % k], 2)
+        vec.tensor_copy(T.yo[:, k * TK:(k + 1) * TK], yp[:, 0:TK]).then_inc(T.sem["v%d" % k], 1)
+
+    for wave in P["waves"][me]:
+        for k in wave:
+            first(k)
+        for k in wave:
+            second(k)
+
+    for k, r in enumerate(order):
+        g.wait_ge(T.sem["v%d" % k], 1)
+        sent += _send(g, T, topo, core, [ranks[r]], T.yin[:, a * TK:(a + 1) * TK],
+                      T.yo[:, k * TK:(k + 1) * TK], T.sem["ya%d" % a])
+    g.wait_ge(T.sem.snt, sent)
+
+
+def rank_program(g, core, T, topo):
+    if "plan" not in _CACHE:
+        _CACHE["plan"] = _plan(T.cores, topo)
+    P = _CACHE["plan"]
+    rank = T.rank_of(core)
+    if rank is not None:
+        _rank(g, core, T, topo, P, rank)
+    elif core in P["site"]:
+        _site(g, core, T, topo, P, P["site"].index(core))

@@ -9,7 +9,7 @@ NBH, NBY = 5, 3
 NE = 8
 
 SCRATCH = {
-    "xs": ("sbuf", [D, TK], "bfloat16"),
+    "xd": ("dram", [D, TK], "bfloat16"),
     "ws": ("sbuf", [D, W], "bfloat16"),
     "yin": ("sbuf", [D, G * TK], "bfloat16"),
     "acc": ("sbuf", [D, (G - 2) * TK], "float32"),
@@ -24,7 +24,8 @@ for _b in range(NBH):
 for _b in range(NBY):
     SCRATCH["yp%d" % _b] = ("psum", [D, 512], "float32")
 
-SEMAPHORES = (["ldx", "ldw", "snt", "st", "w0", "w1"] + ["xa%d" % a for a in range(G)] + ["ya%d" % a for a in range(G)]
+SEMAPHORES = (["ldx", "ldw", "snt", "st", "w0", "w1", "xf", "lx"] + ["xa%d" % a for a in range(G)]
+              + ["ya%d" % a for a in range(G)]
               + ["p%d" % u for u in range(G + 1)] + ["c%d" % k for k in range(G)] + ["q%d" % k for k in range(G)]
               + ["v%d" % k for k in range(G)] + ["s%d" % k for k in range(G)])
 
@@ -41,42 +42,52 @@ def _plan(cores, topo):
         return (topo.host(c), topo.chip(c))
 
     peers = [[k for k in range(N) if rk(ranks[k]) == rk(ranks[i])] for i in range(N)]
-    site = []
+    site, aux = [], []
     for i, s in enumerate(ranks):
         cand = [c for c in range(NSIM) if place(c) == place(s) and c not in ranks
                 and all(topo.may_write(c, ranks[k]) for k in peers[i])]
-        site.append(min(cand, key=lambda c: (topo.die(c) != topo.die(s), c)))
-    partner, direct, fwd = [], [], []
+        cand.sort(key=lambda c: (topo.die(c) != topo.die(s), c))
+        site.append(cand[0])
+        aux.append(cand[1])
+    partner, direct, fa, fb = [], [], [], []
     for i, s in enumerate(ranks):
         partner.append([k for k in range(N) if rk(ranks[k]) != rk(s) and topo.chip(ranks[k]) == topo.chip(s)
                         and topo.may_write(s, site[k])][0])
         a = peers[i].index(i)
         rot = peers[i][a + 1:] + peers[i][:a]
         direct.append([k for k in rot if topo.may_write(s, site[k])])
-        fwd.append([k for k in rot if not topo.may_write(s, site[k])])
+        f = [k for k in rot if not topo.may_write(s, site[k])]
+        if len(f) > 2:
+            h = len(f) // 2
+            fa.append(f[:h])
+            fb.append(f[h:][::-1])
+        else:
+            fa.append(f)
+            fb.append([])
 
     def when(k, i):
         if k == i:
-            return (1, 0)
+            return (-1, 0)
         if i in direct[k]:
-            return (1, 1 + direct[k].index(i))
-        return (2, fwd[k].index(i))
+            return (direct[k].index(i), 0)
+        if i in fa[k]:
+            return (fa[k].index(i), 1)
+        return (fb[k].index(i), 2)
 
     order, waves = [], []
     for i in range(N):
         o = sorted(peers[i], key=lambda k: when(k, i))
         order.append(o)
-        wv = [[n for n, k in enumerate(o) if when(k, i)[0] == 1]]
+        wv = []
         for n, k in enumerate(o):
-            if when(k, i)[0] == 2:
-                if len(wv[-1]) and when(o[wv[-1][-1]], i) == when(k, i):
-                    wv[-1].append(n)
-                else:
-                    wv.append([n])
+            if wv and when(o[wv[-1][-1]], i)[0] == when(k, i)[0]:
+                wv[-1].append(n)
+            else:
+                wv.append([n])
         waves.append(wv)
-    sums = [sorted(peers[r], key=lambda i: (when(r, i)[0], order[i].index(r), when(r, i)[1])) for r in range(N)]
-    return {"peers": peers, "site": site, "partner": partner, "direct": direct, "fwd": fwd, "order": order,
-            "waves": waves, "sums": sums, "rack": [rk(c) for c in ranks]}
+    sums = [sorted(peers[r], key=lambda i: (order[i].index(r), when(r, i))) for r in range(N)]
+    return {"peers": peers, "site": site, "aux": aux, "partner": partner, "direct": direct, "fa": fa, "fb": fb,
+            "order": order, "waves": waves, "sums": sums, "rack": [rk(c) for c in ranks]}
 
 
 def _engines(topo, src, dsts, n):
@@ -104,21 +115,21 @@ def _send(g, T, topo, core, dsts, out_ap, in_ap, sem):
 
 
 def _rank(g, core, T, topo, P, me):
-    ranks = list(T.cores)
     peers, site = P["peers"][me], P["site"]
     a = peers.index(me)
 
-    g.sync.dma_start(T.xs[:], T.x[:]).then_inc(T.sem.ldx, 16)
+    g.sync.dma_start(T.xd[:], T.x[:]).then_inc(T.sem.ldx, 16)
     g.scalar.dma_start(T.ws[:, 0:D], T.w1[:]).then_inc(T.sem.ldw, 16)
     g.sync.dma_start(T.ws[:, D:W], T.w2[:]).then_inc(T.sem.ldw, 16)
 
     g.wait_ge(T.sem.ldx, 16)
-    sent = _send(g, T, topo, core, [site[me]] + [site[k] for k in P["direct"][me]],
-                 T.xall[:, a * TK:(a + 1) * TK], T.xs[:], T.sem["xa%d" % a])
+    sent = _send(g, T, topo, core, [site[me]] + ([P["aux"][me]] if P["fb"][me] else []), T.xd[:], T.xd[:], T.sem.xf)
     g.wait_ge(T.sem.ldw, 32)
     r = P["rack"][me]
     sent += _send(g, T, topo, core, [site[me], site[P["partner"][me]]],
                   T.wts[:, r * W:(r + 1) * W], T.ws[:], T.sem["w%d" % r])
+    sent += _send(g, T, topo, core, [site[k] for k in P["direct"][me]],
+                  T.xall[:, a * TK:(a + 1) * TK], T.xd[:], T.sem["xa%d" % a])
 
     vec = g.vector
     prev = None
@@ -140,9 +151,16 @@ def _rank(g, core, T, topo, P, me):
     g.wait_ge(T.sem.snt, sent)
 
 
+def _forward(g, core, T, topo, P, me, lst):
+    a = P["peers"][me].index(me)
+    g.wait_ge(T.sem.xf, NE)
+    return _send(g, T, topo, core, [P["site"][k] for k in lst], T.xall[:, a * TK:(a + 1) * TK], T.xd[:],
+                 T.sem["xa%d" % a])
+
+
 def _site(g, core, T, topo, P, me):
     ranks = list(T.cores)
-    peers, site, order = P["peers"][me], P["site"], P["order"][me]
+    peers, order = P["peers"][me], P["order"][me]
     a = peers.index(me)
     pe, act, vec = g.tensor, g.scalar, g.vector
     gelu = ActivationFunctionType.Gelu_apprx_tanh
@@ -150,10 +168,11 @@ def _site(g, core, T, topo, P, me):
     slots = [home, 1 - home]
     w1 = [T.wts[:, s * W:s * W + D] for s in slots]
     w2 = [T.wts[:, s * W + D:(s + 1) * W] for s in slots]
+    wsem = [T.sem["w%d" % s] for s in slots]
 
-    g.wait_ge(T.sem["xa%d" % a], NE)
-    sent = _send(g, T, topo, core, [site[k] for k in P["fwd"][me]],
-                 T.xall[:, a * TK:(a + 1) * TK], T.xall[:, a * TK:(a + 1) * TK], T.sem["xa%d" % a])
+    g.sync.wait_ge(T.sem.xf, NE)
+    g.sync.dma_start(T.xall[:, a * TK:(a + 1) * TK], T.xd[:]).then_inc(T.sem.lx, 16)
+    sent = _forward(g, core, T, topo, P, me, P["fa"][me])
 
     unit = [0]
     reader = []
@@ -166,19 +185,21 @@ def _site(g, core, T, topo, P, me):
         return u, T["hp%d" % (u % NBH)]
 
     def first(k):
-        b = peers.index(order[k])
-        x = T.xall[:, b * TK:(b + 1) * TK]
-        pe.wait_ge(T.sem["xa%d" % b], NE)
         ck = T.sem["c%d" % k]
         if k == 0:
+            x = T.xall[:, a * TK:(a + 1) * TK]
+            pe.wait_ge(T.sem.lx, 16)
             for e in range(2):
-                pe.wait_ge(T.sem["w%d" % slots[e]], NE)
+                pe.wait_ge(wsem[e], NE)
                 u, hp = bank()
                 reader.append((ck, 2))
                 pe.matmul(hp[:, 0:TK], w1[e], x, True, True).then_inc(T.sem["p%d" % u], 1)
                 act.wait_ge(T.sem["p%d" % u], 1)
                 act.activation(T.hs[:, e * TK:(e + 1) * TK], hp[:, 0:TK], gelu).then_inc(ck, 1)
         else:
+            b = peers.index(order[k])
+            x = T.xall[:, b * TK:(b + 1) * TK]
+            pe.wait_ge(T.sem["xa%d" % b], NE)
             u, hp = bank()
             reader.append((ck, 1))
             for e in range(2):
@@ -219,3 +240,6 @@ def rank_program(g, core, T, topo):
         _rank(g, core, T, topo, P, rank)
     elif core in P["site"]:
         _site(g, core, T, topo, P, P["site"].index(core))
+    elif core in P["aux"] and P["fb"][P["aux"].index(core)]:
+        me = P["aux"].index(core)
+        g.wait_ge(T.sem.snt, _forward(g, core, T, topo, P, me, P["fb"][me]))

from concourse.bass import DstId, RemoteDMATransfer
from concourse.mybir import ActivationFunctionType, AluOpType

N, TK, D = 12, 64, 128
NSIM = 512
W = 2 * D
G = 6
NBH, NBY = 5, 3
NE = 8

SCRATCH = {
    "xd": ("dram", [D, TK], "bfloat16"),
    "ws": ("sbuf", [D, W], "bfloat16"),
    "yin": ("sbuf", [D, G * TK], "bfloat16"),
    "acc": ("sbuf", [D, (G - 2) * TK], "float32"),
    "ys": ("sbuf", [D, TK], "bfloat16"),
    "xall": ("sbuf", [D, G * TK], "bfloat16"),
    "wts": ("sbuf", [D, 2 * W], "bfloat16"),
    "hs": ("sbuf", [D, G * 2 * TK], "bfloat16"),
    "yo": ("sbuf", [D, G * TK], "bfloat16"),
}
for _b in range(NBH):
    SCRATCH["hp%d" % _b] = ("psum", [D, 512], "float32")
for _b in range(NBY):
    SCRATCH["yp%d" % _b] = ("psum", [D, 512], "float32")

SEMAPHORES = (["ldx", "ldw", "snt", "st", "w0", "w1", "xf", "lx"] + ["xa%d" % a for a in range(G)]
              + ["ya%d" % a for a in range(G)]
              + ["p%d" % u for u in range(G + 1)] + ["c%d" % k for k in range(G)] + ["q%d" % k for k in range(G)]
              + ["v%d" % k for k in range(G)] + ["s%d" % k for k in range(G)])

_CACHE = {}


def _plan(cores, topo):
    ranks = list(cores)

    def rk(c):
        return topo.rack(topo.host(c))

    def place(c):
        return (topo.host(c), topo.chip(c))

    peers = [[k for k in range(N) if rk(ranks[k]) == rk(ranks[i])] for i in range(N)]
    site, aux = [], []
    for i, s in enumerate(ranks):
        cand = [c for c in range(NSIM) if place(c) == place(s) and c not in ranks
                and all(topo.may_write(c, ranks[k]) for k in peers[i])]
        cand.sort(key=lambda c: (topo.die(c) != topo.die(s), c))
        site.append(cand[0])
        aux.append(cand[1])
    partner, direct, fa, fb = [], [], [], []
    for i, s in enumerate(ranks):
        partner.append([k for k in range(N) if rk(ranks[k]) != rk(s) and topo.chip(ranks[k]) == topo.chip(s)
                        and topo.may_write(s, site[k])][0])
        a = peers[i].index(i)
        rot = peers[i][a + 1:] + peers[i][:a]
        direct.append([k for k in rot if topo.may_write(s, site[k])])
        f = [k for k in rot if not topo.may_write(s, site[k])]
        if len(f) > 2:
            h = len(f) // 2
            fa.append(f[:h])
            fb.append(f[h:][::-1])
        else:
            fa.append(f)
            fb.append([])

    def when(k, i):
        if k == i:
            return (-1, 0)
        if i in direct[k]:
            return (direct[k].index(i), 0)
        if i in fa[k]:
            return (fa[k].index(i), 1)
        return (fb[k].index(i), 2)

    order, waves = [], []
    for i in range(N):
        o = sorted(peers[i], key=lambda k: when(k, i))
        order.append(o)
        wv = []
        for n, k in enumerate(o):
            if wv and when(o[wv[-1][-1]], i)[0] == when(k, i)[0]:
                wv[-1].append(n)
            else:
                wv.append([n])
        waves.append(wv)
    sums = [sorted(peers[r], key=lambda i: (order[i].index(r), when(r, i))) for r in range(N)]
    return {"peers": peers, "site": site, "aux": aux, "partner": partner, "direct": direct, "fa": fa, "fb": fb,
            "order": order, "waves": waves, "sums": sums, "rack": [rk(c) for c in ranks]}


def _engines(topo, src, dsts, n):
    allowed = topo.mask(src, dsts[0])
    for d in dsts[1:]:
        allowed &= topo.mask(src, d)
    out, b, k = 0, 0, 0
    while k < n:
        if (allowed >> b) & 1:
            out |= 1 << b
            k += 1
        b += 1
    return out


def _send(g, T, topo, core, dsts, out_ap, in_ap, sem):
    ids = []
    for d in dsts:
        rid, pid = topo.addr(d, core)
        ids.append(DstId(rid=rid, pnc=pid))
    g.remote_dma_fused([RemoteDMATransfer(dst_ids=ids, dma_engine_mask=_engines(topo, core, dsts, NE), remote_sem=sem,
                                          srcs=[in_ap], dsts=[out_ap for _ in dsts], alu_op=0)],
                       local_sem=T.sem.snt)
    return NE


def _rank(g, core, T, topo, P, me):
    peers, site = P["peers"][me], P["site"]
    a = peers.index(me)

    g.sync.dma_start(T.xd[:], T.x[:]).then_inc(T.sem.ldx, 16)
    g.scalar.dma_start(T.ws[:, 0:D], T.w1[:]).then_inc(T.sem.ldw, 16)
    g.sync.dma_start(T.ws[:, D:W], T.w2[:]).then_inc(T.sem.ldw, 16)

    g.wait_ge(T.sem.ldx, 16)
    sent = _send(g, T, topo, core, [site[me]] + ([P["aux"][me]] if P["fb"][me] else []), T.xd[:], T.xd[:], T.sem.xf)
    g.wait_ge(T.sem.ldw, 32)
    r = P["rack"][me]
    sent += _send(g, T, topo, core, [site[me], site[P["partner"][me]]],
                  T.wts[:, r * W:(r + 1) * W], T.ws[:], T.sem["w%d" % r])
    sent += _send(g, T, topo, core, [site[k] for k in P["direct"][me]],
                  T.xall[:, a * TK:(a + 1) * TK], T.xd[:], T.sem["xa%d" % a])

    vec = g.vector
    prev = None
    for n, i in enumerate(P["sums"][me]):
        b = peers.index(i)
        part = T.yin[:, b * TK:(b + 1) * TK]
        vec.wait_ge(T.sem["ya%d" % b], NE)
        if n == 0:
            prev = part
            continue
        if n >= 2:
            vec.wait_ge(T.sem["s%d" % (n - 1)], 1)
        out = T.ys[:] if n == G - 1 else T.acc[:, (n - 1) * TK:n * TK]
        vec.tensor_tensor(out, prev, part, AluOpType.add).then_inc(T.sem["s%d" % n], 1)
        prev = out
    g.sync.wait_ge(T.sem["s%d" % (G - 1)], 1)
    g.sync.dma_start(T.y[:], T.ys[:]).then_inc(T.sem.st, 16)
    g.sync.wait_ge(T.sem.st, 16)
    g.wait_ge(T.sem.snt, sent)


def _forward(g, core, T, topo, P, me, lst):
    a = P["peers"][me].index(me)
    g.wait_ge(T.sem.xf, NE)
    return _send(g, T, topo, core, [P["site"][k] for k in lst], T.xall[:, a * TK:(a + 1) * TK], T.xd[:],
                 T.sem["xa%d" % a])


def _site(g, core, T, topo, P, me):
    ranks = list(T.cores)
    peers, order = P["peers"][me], P["order"][me]
    a = peers.index(me)
    pe, act, vec = g.tensor, g.scalar, g.vector
    gelu = ActivationFunctionType.Gelu_apprx_tanh
    home = P["rack"][me]
    slots = [home, 1 - home]
    w1 = [T.wts[:, s * W:s * W + D] for s in slots]
    w2 = [T.wts[:, s * W + D:(s + 1) * W] for s in slots]
    wsem = [T.sem["w%d" % s] for s in slots]

    g.sync.wait_ge(T.sem.xf, NE)
    g.sync.dma_start(T.xall[:, a * TK:(a + 1) * TK], T.xd[:]).then_inc(T.sem.lx, 16)
    sent = _forward(g, core, T, topo, P, me, P["fa"][me])

    unit = [0]
    reader = []

    def bank():
        u = unit[0]
        unit[0] += 1
        if u >= NBH:
            pe.wait_ge(*reader[u - NBH])
        return u, T["hp%d" % (u % NBH)]

    def first(k):
        ck = T.sem["c%d" % k]
        if k == 0:
            x = T.xall[:, a * TK:(a + 1) * TK]
            pe.wait_ge(T.sem.lx, 16)
            for e in range(2):
                pe.wait_ge(wsem[e], NE)
                u, hp = bank()
                reader.append((ck, 2))
                pe.matmul(hp[:, 0:TK], w1[e], x, True, True).then_inc(T.sem["p%d" % u], 1)
                act.wait_ge(T.sem["p%d" % u], 1)
                act.activation(T.hs[:, e * TK:(e + 1) * TK], hp[:, 0:TK], gelu).then_inc(ck, 1)
        else:
            b = peers.index(order[k])
            x = T.xall[:, b * TK:(b + 1) * TK]
            pe.wait_ge(T.sem["xa%d" % b], NE)
            u, hp = bank()
            reader.append((ck, 1))
            for e in range(2):
                pe.matmul(hp[:, e * TK:(e + 1) * TK], w1[e], x, True, True).then_inc(T.sem["p%d" % u], 1)
            act.wait_ge(T.sem["p%d" % u], 2)
            act.activation(T.hs[:, 2 * k * TK:(2 * k + 2) * TK], hp[:, 0:2 * TK], gelu).then_inc(ck, 1)

    def second(k):
        pe.wait_ge(T.sem["c%d" % k], 2 if k == 0 else 1)
        if k >= NBY:
            pe.wait_ge(T.sem["v%d" % (k - NBY)], 1)
        yp = T["yp%d" % (k % NBY)]
        for e in range(2):
            pe.matmul(yp[:, 0:TK], w2[e], T.hs[:, (2 * k + e) * TK:(2 * k + e + 1) * TK],
                      e == 0, e == 1).then_inc(T.sem["q%d" % k], 1)
        vec.wait_ge(T.sem["q%d" % k], 2)
        vec.tensor_copy(T.yo[:, k * TK:(k + 1) * TK], yp[:, 0:TK]).then_inc(T.sem["v%d" % k], 1)

    for wave in P["waves"][me]:
        for k in wave:
            first(k)
        for k in wave:
            second(k)

    for k, r in enumerate(order):
        g.wait_ge(T.sem["v%d" % k], 1)
        sent += _send(g, T, topo, core, [ranks[r]], T.yin[:, a * TK:(a + 1) * TK],
                      T.yo[:, k * TK:(k + 1) * TK], T.sem["ya%d" % a])
    g.wait_ge(T.sem.snt, sent)


def rank_program(g, core, T, topo):
    if "plan" not in _CACHE:
        _CACHE["plan"] = _plan(T.cores, topo)
    P = _CACHE["plan"]
    rank = T.rank_of(core)
    if rank is not None:
        _rank(g, core, T, topo, P, rank)
    elif core in P["site"]:
        _site(g, core, T, topo, P, P["site"].index(core))
    elif core in P["aux"] and P["fb"][P["aux"].index(core)]:
        me = P["aux"].index(core)
        g.wait_ge(T.sem.snt, _forward(g, core, T, topo, P, me, P["fb"][me]))
